import numpy as np
import ml_dtypes


def mxq(x, axis, fmt="e4m3"):
    dtype, down = {"e4m3": (ml_dtypes.float8_e4m3fn, 7), "e5m2": (ml_dtypes.float8_e5m2, 14)}[fmt]
    v = np.moveaxis(np.asarray(x, np.float32).astype(ml_dtypes.bfloat16).astype(np.float64), axis, -1)
    blocks = v.reshape(v.shape[:-1] + (-1, 32))
    amax = np.abs(blocks).max(-1, keepdims=True)
    byte = np.maximum(np.where(amax > 0, np.frexp(amax)[1] - 1 + 127, 0) - down, 1)
    scale = np.exp2(byte - 127.0)
    codes = (blocks / scale).astype(np.float32).astype(dtype).astype(np.float64)
    return np.moveaxis((codes * scale).reshape(v.shape), -1, axis)


WIDE = False


def mx_kscale(k):
    if not WIDE:
        return np.ones(k)
    levels = np.array([10, -10, 5, -5, 0])
    if k % 512:
        return np.exp2(np.random.permutation(np.resize(levels, k // 32))).repeat(32)
    a = np.empty((k // 512, 16))
    for p in range(k // 512):
        a[p, :8] = np.random.permutation(np.resize(levels, 8))
        for g in range(8):
            far = levels[np.abs(levels - a[p, g]) >= 10]
            a[p, g + 8] = far[np.random.randint(len(far))]
    return np.exp2(a.ravel()).repeat(32)


def f64(x):
    return np.asarray(x).astype(np.float64)


def striped(idx):
    return np.tile(idx.reshape(-1, 16).T, (8, 1)).astype(np.uint16)


def unstriped(offs):
    return offs[:16].T.reshape(-1).astype(np.int64)


E2M1 = np.array([0.0, 0.5, 1.0, 1.5, 2.0, 3.0, 4.0, 6.0, -0.0, -0.5, -1.0, -1.5, -2.0, -3.0, -4.0, -6.0])


def pack_weight(w, fmt):
    k, n = w.shape
    w = f64(np.asarray(w, np.float32).astype(ml_dtypes.bfloat16)).reshape(k // 32, 32, n)
    amax = np.abs(w).max(1)
    if fmt == "e4m3":
        byte = np.frexp(amax)[1] - 1 + 127 - 7
    else:
        mant, ex = np.frexp(amax / 6.0)
        byte = np.where(mant > 0.5, ex, ex - 1) + 127
    byte = np.clip(np.where(amax > 0, byte, 1), 1, 254)
    scaled = (w * np.exp2(127.0 - byte)[:, None, :]).reshape(k, n).astype(np.float32)
    by_word = np.ascontiguousarray(scaled.reshape(k // 512, 128, 4, n).transpose(0, 1, 3, 2))
    if fmt == "e4m3":
        words = by_word.astype(ml_dtypes.float8_e4m3fn).view(np.uint8)
    else:
        c = by_word.astype(ml_dtypes.float4_e2m1fn).view(np.uint8) & 0xF
        words = (c[..., 0::2] | (c[..., 1::2] << 4)).reshape(k // 512, 128, 2 * n)
    return np.ascontiguousarray(words), np.ascontiguousarray(byte.astype(np.uint8).reshape(k // 512, 16, n))


def unpack_weight(words, scales, fmt):
    g, _, n = scales.shape
    words = np.ascontiguousarray(words).reshape(g, 128, n, -1)
    if fmt == "e4m3":
        vals = words.view(ml_dtypes.float8_e4m3fn).astype(np.float64)
    else:
        nib = np.empty((g, 128, n, 4), np.uint8)
        nib[..., 0::2] = words & 0xF
        nib[..., 1::2] = words >> 4
        vals = E2M1[nib]
    vals = vals * np.repeat(np.exp2(scales.astype(np.float64) - 127.0), 8, axis=1)[..., None]
    return vals.transpose(0, 1, 3, 2).reshape(g * 512, n)


def gelu(v):
    return 0.5 * v * (1.0 + np.tanh(np.sqrt(2.0 / np.pi) * (v + 0.044715 * v**3)))


K, H, T, S, T2, P = 1024, 512, 2048, 1024, 2048, 1024

def setup_inputs():
    n = np.random.standard_normal
    s = mx_kscale(K)[:, None]
    u = mx_kscale(H)[:, None]
    tab_words, tab_scales = pack_weight(n((K, T)) * s, "e4m3")
    wn_words, wn_scales = pack_weight(2.0 * n((K, H)) / np.sqrt(K) / s * u.T, "e2m1")
    return {
        "tab_words": tab_words, "tab_scales": tab_scales,
        "offs": striped(np.random.permutation(T)[:S]),
        "wn_words": wn_words, "wn_scales": wn_scales,
        "wd": (1.5 * n((K, H)) / np.sqrt(K) / s).astype(np.float32),
        "page0": (n((H, T2)) * u).astype(np.float32),
        "wgs": np.exp(0.3 * n((128, S))).astype(np.float32),
        "offs2": striped(np.random.permutation(T2)[:S]),
        "offs3": striped(np.random.permutation(T2)[:P]),
        "base": (n((H, P)) * u).astype(np.float32),
        "wr": (n((H, H)) / np.sqrt(H) / u * u.T).astype(np.float32),
        "wgo": np.exp(0.3 * n((128, P))).astype(np.float32),
        "offs4": striped(np.random.permutation(T2)[:P]),
    }

def reference(tab_words, tab_scales, offs, wn_words, wn_scales, wd, page0, wgs, offs2, offs3, base, wr, wgo, offs4):
    v = unpack_weight(tab_words, tab_scales, "e4m3")[:, unstriped(offs)]
    num = unpack_weight(wn_words, wn_scales, "e2m1").T @ v
    den = mxq(f64(wd), 0, "e4m3").T @ v
    h = num / (1.0 + np.abs(den))
    page = f64(page0).copy()
    page[:, unstriped(offs2)] = np.tile(f64(wgs), (H // 128, 1)) * h
    x = page[:, unstriped(offs3)]
    z = np.maximum(x, f64(base))
    y = mxq(f64(wr), 0, "e4m3").T @ mxq(z, 0, "e4m3")
    y = np.minimum(y, x)
    page[:, unstriped(offs4)] = np.tile(f64(wgo), (H // 128, 1)) * y
    return page

@@ -1,0 +1,271 @@
+from contextlib import ExitStack
+
+import concourse.mybir as mybir
+from concourse.masks import make_identity
+
+K, H, T, S, T2, NP = 1024, 512, 2048, 1024, 2048, 1024
+FLOPS = 2 * (2 * K * H * S) + 2 * H * H * NP
+
+F32 = mybir.dt.float32
+BF16 = mybir.dt.bfloat16
+I32 = mybir.dt.int32
+U32 = mybir.dt.uint32
+U16 = mybir.dt.uint16
+U8 = mybir.dt.uint8
+FP8X4 = mybir.dt.float8_e4m3fn_x4
+FP4X4 = mybir.dt.float4_e2m1fn_x4
+ACT = mybir.ActivationFunctionType
+ALU = mybir.AluOpType
+
+P = 128
+PACK = 4
+PASSES = K // (P * PACK)
+ROWT = H // P
+HALF = 512
+LCOL = HALF // 16
+
+
+def tile_list_surge_margin_page_kernel(
+    tc, tab_words, tab_scales, offs, wn_words, wn_scales, wd, page0, wgs, offs2, offs3, base, wr, wgo, offs4, out
+):
+    nc = tc.nc
+    with ExitStack() as ctx:
+        lists = ctx.enter_context(tc.tile_pool(name="lists", bufs=1))
+        keep = ctx.enter_context(tc.tile_pool(name="keep", bufs=1))
+        ring = ctx.enter_context(tc.tile_pool(name="ring", bufs=2))
+        psum = ctx.enter_context(tc.psum_pool(name="psum", bufs=2))
+
+        def kept(shape, dtype, name, tag=""):
+            return keep.tile(shape, dtype, name=name, tag=tag or name, align_bytes=64)
+
+        def load_list(src, name):
+            tile = lists.tile([P, S // 16], U16, name=name)
+            nc.sync.dma_start(tile[:], src)
+            return tile
+
+        def half_of(lst, h):
+            return lst[:, h * LCOL : (h + 1) * LCOL]
+
+        tab_sc = kept([P, T], U8, "tab_sc")
+        nc.vector.memset(tab_sc[:].bitcast(I32), 0)
+        wn_sc = kept([P, PASSES, H], U8, "wn_sc")
+        nc.vector.memset(wn_sc[:].rearrange("p a c -> p (a c)").bitcast(I32), 0)
+        v_sc1 = kept([P, S], U8, "v_sc1")
+        nc.vector.memset(v_sc1[:].bitcast(I32), 0)
+
+        idx = load_list(offs, "idx")
+        for q in range(4):
+            nc.sync.dma_start(
+                tab_sc[32 * q : 32 * q + 8, :].bitcast(I32), tab_scales[:, 4 * q : 4 * q + 4, :].bitcast(I32)
+            )
+        idx2 = load_list(offs2, "idx2")
+        idx3 = load_list(offs3, "idx3")
+        idx4 = load_list(offs4, "idx4")
+        wn_w = kept([P, PASSES, 2 * H], U8, "wn_w")
+        tab_w = [kept([P, T], I32, "tab_w%d" % a) for a in range(PASSES)]
+        wd_rows = wd.rearrange("(a p j) c -> a p j c", a=PASSES, j=PACK)
+        wd_raw = [[kept([P, PACK, 2 * P], F32, "wd_raw%d_%d" % (s, a)) for a in range(PASSES)] for s in range(2)]
+        nc.sync.dma_start(tab_w[0][:], tab_words[0].rearrange("p t i -> p (t i)").bitcast(I32))
+        nc.sync.dma_start(wn_w[:].bitcast(I32), wn_words.rearrange("a p c -> p a c").bitcast(I32))
+        for a in range(PASSES):
+            nc.sync.dma_start(wd_raw[0][a][:], wd_rows[a, :, :, 0 : 2 * P])
+        nc.sync.dma_start(tab_w[1][:], tab_words[1].rearrange("p t i -> p (t i)").bitcast(I32))
+        for q in range(4):
+            nc.sync.dma_start(
+                wn_sc[32 * q : 32 * q + 4, :, :].bitcast(I32),
+                wn_scales[:, 4 * q : 4 * q + 4, :].rearrange("a r c -> r a c").bitcast(I32),
+            )
+
+        pages = [kept([P, T2], F32, "page%d" % t) for t in range(ROWT)]
+        nc.sync.dma_start(pages[0][:], page0[0:P, :])
+        wgs_sb = kept([P, S], F32, "wgs_sb", tag="wgs_x1")
+        nc.sync.dma_start(wgs_sb[:], wgs)
+        for a in range(PASSES):
+            nc.sync.dma_start(wd_raw[1][a][:], wd_rows[a, :, :, 2 * P : H])
+        nc.sync.dma_start(pages[1][:], page0[P : 2 * P, :])
+        base_sb = [kept([P, ROWT, HALF], F32, "base%d" % h) for h in range(2)]
+        base_rows = base.rearrange("(t p) j -> p t j", p=P)
+        nc.sync.dma_start(base_sb[0][:], base_rows[:, :, 0:HALF])
+        for t in range(2, ROWT):
+            nc.sync.dma_start(pages[t][:], page0[t * P : (t + 1) * P, :])
+        wr_raw = kept([P, PACK, H], F32, "wr_raw")
+        nc.sync.dma_start(wr_raw[:], wr.rearrange("(p j) c -> p j c", j=PACK))
+        nc.sync.dma_start(base_sb[1][:], base_rows[:, :, HALF:NP])
+        wgo_sb = kept([P, NP], F32, "wgo_sb")
+        nc.sync.dma_start(wgo_sb[:], wgo)
+
+        ident_bf = kept([P, P], BF16, "ident_bf")
+        make_identity(nc, ident_bf[:])
+        ident_f = kept([P, P], F32, "ident_f")
+        make_identity(nc, ident_f[:])
+
+        v_sc = kept([P, S], U8, "v_sc")
+        nc.vector.tensor_copy(v_sc[:], tab_sc[:].indirect(idx[:]))
+        nc.scalar.dma_start(v_sc1[0:112, :].bitcast(I32), v_sc[4:116, :].bitcast(I32))
+        v_w = [[kept([P, HALF], U32, "v_w%d_%d" % (a, h)) for h in range(2)] for a in range(PASSES)]
+        for a in range(PASSES):
+            for h in range(2):
+                nc.vector.tensor_copy(v_w[a][h][:], tab_w[a][:].bitcast(U32).indirect(half_of(idx, h)))
+
+        def interleave(dst, src):
+            nc.scalar.copy(
+                dst.rearrange("p (c i) j -> p c j i", i=4),
+                src.rearrange("p j (c i) -> p c j i", i=4),
+            )
+
+        def quantise(src, width, name):
+            codes = kept([P, width], U32, name + "_codes")
+            scales = kept([P, width], U8, name + "_scales")
+            nc.vector.quantize_mx(out=codes[:].bitcast(FP8X4), scales=scales[:], in_=src)
+            return codes, scales
+
+        def sums(t, h, wd_c, wd_s):
+            cols = slice(h * HALF, (h + 1) * HALF)
+            den = psum.tile([P, HALF], F32, name="den", tag="acc_a")
+            for a in range(PASSES):
+                nc.tensor.matmul_mx(
+                    out=den[:],
+                    lhsT=wd_c[:, a * P : (a + 1) * P].bitcast(FP8X4),
+                    lhsT_scale=wd_s[:, a * P : (a + 1) * P],
+                    rhs=v_w[a][h][:].bitcast(FP8X4),
+                    rhs_scale=v_sc[4 * a : P, cols],
+                    start=(a == 0),
+                    stop=(a == PASSES - 1),
+                )
+            num = psum.tile([P, HALF], F32, name="num", tag="acc_b")
+            for a in range(PASSES):
+                nc.tensor.matmul_mx(
+                    out=num[:],
+                    lhsT=wn_w[:, a, 2 * t * P : 2 * (t + 1) * P].bitcast(FP4X4),
+                    lhsT_scale=wn_sc[:, a, t * P : (t + 1) * P],
+                    rhs=v_w[a][h][:].bitcast(FP8X4),
+                    rhs_scale=(v_sc, v_sc1)[a][:, cols],
+                    start=(a == 0),
+                    stop=(a == PASSES - 1),
+                )
+            return num, den
+
+        def halves(tile):
+            return [tile[:, h * HALF : (h + 1) * HALF] for h in range(2)]
+
+        x = [[None] * ROWT, [None] * ROWT]
+        z = [kept([P, ROWT, HALF], BF16, "z0"), None]
+        turned = [None, None]
+
+        def fetch(t, h, dst):
+            x[h][t] = dst
+            nc.vector.tensor_copy(dst, pages[t][:].indirect(half_of(idx3, h)))
+
+        def hold_up(t, h):
+            nc.vector.tensor_tensor(z[h][:, t, :], x[h][t], base_sb[h][:, t, :], ALU.max)
+            for g in range(2):
+                if t == 0:
+                    turned[g] = psum.tile([P, 2, H], BF16, name="turned", tag="turned")
+                for b in range(2):
+                    j0 = (2 * g + b) * P
+                    nc.tensor.transpose(turned[g][:, b, t * P : (t + 1) * P], z[h][:, t, j0 : j0 + P], ident_bf[:])
+
+        def regroup(h):
+            z_il = kept([P, HALF * PACK], BF16, "z_il%d" % h)
+            for g in range(2):
+                z_t = ring.tile([P, 2, H], BF16, name="z_t", align_bytes=64)
+                nc.scalar.copy(z_t[:], turned[g][:])
+                back = psum.tile([P, 2, 2, P], F32, name="back", tag="back")
+                for b in range(2):
+                    words = z_t[:, b, :].bitcast(F32)
+                    for u in range(2):
+                        nc.tensor.transpose(back[:, b, u, :], words[:, u : H // 2 : 2], ident_f[:])
+                nc.scalar.copy(
+                    z_il[:, g * 1024 : (g + 1) * 1024].bitcast(F32).rearrange("p (b j u) -> p b j u", b=2, u=2),
+                    back[:].rearrange("p b u j -> p b j u"),
+                )
+            return quantise(z_il[:], HALF, "z%d" % h)
+
+        for t in range(ROWT):
+            wd_bf = ring.tile([P, PASSES, P, PACK], BF16, name="wd_bf", align_bytes=64)
+            for a in range(PASSES):
+                interleave(wd_bf[:, a, :, :], wd_raw[t // 2][a][:, :, (t % 2) * P : (t % 2 + 1) * P])
+            wd_c, wd_s = quantise(wd_bf[:].rearrange("p a c j -> p (a c j)"), PASSES * P, "wd%d" % t)
+            hh = ring.tile([P, S], F32, name="hh")
+            mag = ring.tile([P, S], F32, name="mag")
+            root = ring.tile([P, S], F32, name="root")
+            recip = kept([P, S], F32, "recip%d" % t)
+            if t == 0:
+                for h in range(2):
+                    num, den = sums(t, h, wd_c, wd_s)
+                    nc.scalar.activation(halves(mag)[h], den[:], ACT.Abs)
+                    nc.scalar.activation(halves(root)[h], halves(mag)[h], ACT.Abs_reciprocal_sqrt, bias=1.0)
+                    nc.scalar.activation(halves(recip)[h], halves(root)[h], ACT.Square)
+                    nc.vector.tensor_tensor(halves(hh)[h], num[:], halves(recip)[h], ALU.mult)
+                    nc.vector.tensor_tensor(
+                        pages[t][:].indirect(half_of(idx2, h)), halves(hh)[h], halves(wgs_sb)[h], ALU.mult
+                    )
+            else:
+                nums = []
+                for h in range(2):
+                    num, den = sums(t, h, wd_c, wd_s)
+                    nums.append(num)
+                    nc.scalar.activation(halves(mag)[h], den[:], ACT.Abs)
+                nc.scalar.activation(root[:], mag[:], ACT.Abs_reciprocal_sqrt, bias=1.0)
+                nc.scalar.activation(recip[:], root[:], ACT.Square)
+                for h in range(2):
+                    nc.vector.tensor_tensor(halves(hh)[h], nums[h][:], halves(recip)[h], ALU.mult)
+                fetch(t - 1, 0, halves(recip)[0])
+                nc.vector.tensor_tensor(pages[t][:].indirect(idx2[:]), hh[:], wgs_sb[:], ALU.mult)
+                hold_up(t - 1, 0)
+
+        wr_bf = kept([P, H, PACK], BF16, "wr_bf")
+        interleave(wr_bf[:], wr_raw[:])
+        wr_c, wr_s = quantise(wr_bf[:].rearrange("p c j -> p (c j)"), H, "wr")
+
+        x_last = kept([P, HALF], F32, "x_last")
+        x_late = kept([P, ROWT, HALF], F32, "x_late", tag="wgs_x1")
+        fetch(ROWT - 1, 0, x_last[:])
+        fetch(0, 1, x_late[:, 0, :])
+        hold_up(ROWT - 1, 0)
+        for t in range(1, ROWT):
+            fetch(t, 1, x_late[:, t, :])
+        zq = [regroup(0), None]
+        z[1] = kept([P, ROWT, HALF], BF16, "z1", tag="z_il0")
+        for t in range(ROWT):
+            hold_up(t, 1)
+
+        lows = [kept([P, NP], F32, "low%d" % t) for t in range(ROWT)]
+
+        def rescore(t, h):
+            z_c, z_s = zq[h]
+            y = psum.tile([P, HALF], F32, name="y", tag=("acc_a", "acc_b")[t % 2])
+            nc.tensor.matmul_mx(
+                out=y[:],
+                lhsT=wr_c[:, t * P : (t + 1) * P].bitcast(FP8X4),
+                lhsT_scale=wr_s[:, t * P : (t + 1) * P],
+                rhs=z_c[:].bitcast(FP8X4),
+                rhs_scale=z_s[:],
+                start=True,
+                stop=True,
+            )
+            nc.vector.tensor_tensor(halves(lows[t])[h], y[:], x[h][t], ALU.min)
+
+        def put_first_tile(h):
+            nc.vector.tensor_tensor(
+                pages[0][:].indirect(half_of(idx4, h)), halves(lows[0])[h], halves(wgo_sb)[h], ALU.mult
+            )
+
+        def store(t):
+            nc.sync.dma_start(out[t * P : (t + 1) * P, :], pages[t][:])
+
+        rescore(0, 0)
+        rescore(1, 0)
+        put_first_tile(0)
+        zq[1] = regroup(1)
+        rescore(2, 0)
+        rescore(3, 0)
+        rescore(0, 1)
+        rescore(1, 1)
+        put_first_tile(1)
+        store(0)
+        for t in range(1, ROWT):
+            if t + 1 < ROWT:
+                rescore(t + 1, 1)
+            nc.vector.tensor_tensor(pages[t][:].indirect(idx4[:]), lows[t][:], wgo_sb[:], ALU.mult)
+            store(t)

@@ -22,7 +22,9 @@ PACK = 4
 PASSES = K // (P * PACK)
 ROWT = H // P
 HALF = 512
-LCOL = HALF // 16
+QUARTER = HALF // 2
+HALVES = ((0, HALF), (HALF, S))
+FIRST_CUTS = ((0, QUARTER), (QUARTER, HALF), (HALF, S))
 
 
 def tile_list_surge_margin_page_kernel(
@@ -43,8 +45,11 @@ def tile_list_surge_margin_page_kernel(
             nc.sync.dma_start(tile[:], src)
             return tile
 
+        def entries(lst, c0, c1):
+            return lst[:, c0 // 16 : c1 // 16]
+
         def half_of(lst, h):
-            return lst[:, h * LCOL : (h + 1) * LCOL]
+            return entries(lst, h * HALF, (h + 1) * HALF)
 
         tab_sc = kept([P, T], U8, "tab_sc")
         nc.vector.memset(tab_sc[:].bitcast(I32), 0)
@@ -61,14 +66,21 @@ def tile_list_surge_margin_page_kernel(
         idx2 = load_list(offs2, "idx2")
         idx3 = load_list(offs3, "idx3")
         idx4 = load_list(offs4, "idx4")
-        wn_w = kept([P, PASSES, 2 * H], U8, "wn_w")
-        tab_w = [kept([P, T], I32, "tab_w%d" % a) for a in range(PASSES)]
+        wn_w = kept([P, PASSES, 2 * H], U8, "wn_w", tag="wn_wr")
+        tab_w = [kept([P, T], I32, "tab_w%d" % a, tag="tab%d" % a) for a in range(PASSES)]
         wd_rows = wd.rearrange("(a p j) c -> a p j c", a=PASSES, j=PACK)
-        wd_raw = [[kept([P, PACK, 2 * P], F32, "wd_raw%d_%d" % (s, a)) for a in range(PASSES)] for s in range(2)]
+        wd_raw = [kept([P, PASSES, PACK, P], F32, "wd_raw%d" % t)[:] for t in range(2)]
+
+        def load_wd_early(t):
+            for a in range(PASSES):
+                nc.sync.dma_start(wd_raw[t][:, a, :, :], wd_rows[a, :, :, t * P : (t + 1) * P])
+
+        def load_wn(a):
+            nc.sync.dma_start(wn_w[:, a, :].bitcast(I32), wn_words[a].bitcast(I32))
+
         nc.sync.dma_start(tab_w[0][:], tab_words[0].rearrange("p t i -> p (t i)").bitcast(I32))
-        nc.sync.dma_start(wn_w[:].bitcast(I32), wn_words.rearrange("a p c -> p a c").bitcast(I32))
-        for a in range(PASSES):
-            nc.sync.dma_start(wd_raw[0][a][:], wd_rows[a, :, :, 0 : 2 * P])
+        load_wd_early(0)
+        load_wn(0)
         nc.sync.dma_start(tab_w[1][:], tab_words[1].rearrange("p t i -> p (t i)").bitcast(I32))
         for q in range(4):
             nc.sync.dma_start(
@@ -76,36 +88,50 @@ def tile_list_surge_margin_page_kernel(
                 wn_scales[:, 4 * q : 4 * q + 4, :].rearrange("a r c -> r a c").bitcast(I32),
             )
 
-        pages = [kept([P, T2], F32, "page%d" % t) for t in range(ROWT)]
-        nc.sync.dma_start(pages[0][:], page0[0:P, :])
-        wgs_sb = kept([P, S], F32, "wgs_sb", tag="wgs_x1")
-        nc.sync.dma_start(wgs_sb[:], wgs)
-        for a in range(PASSES):
-            nc.sync.dma_start(wd_raw[1][a][:], wd_rows[a, :, :, 2 * P : H])
-        nc.sync.dma_start(pages[1][:], page0[P : 2 * P, :])
-        base_sb = [kept([P, ROWT, HALF], F32, "base%d" % h) for h in range(2)]
-        base_rows = base.rearrange("(t p) j -> p t j", p=P)
-        nc.sync.dma_start(base_sb[0][:], base_rows[:, :, 0:HALF])
-        for t in range(2, ROWT):
+        load_wn(1)
+        pages = [None] * ROWT
+
+        def load_page(t, tag):
+            pages[t] = kept([P, T2], F32, "page%d" % t, tag=tag)
             nc.sync.dma_start(pages[t][:], page0[t * P : (t + 1) * P, :])
-        wr_raw = kept([P, PACK, H], F32, "wr_raw")
-        nc.sync.dma_start(wr_raw[:], wr.rearrange("(p j) c -> p j c", j=PACK))
-        nc.sync.dma_start(base_sb[1][:], base_rows[:, :, HALF:NP])
-        wgo_sb = kept([P, NP], F32, "wgo_sb")
-        nc.sync.dma_start(wgo_sb[:], wgo)
+
+        base_sb = [None, None]
+        base_rows = base.rearrange("(t p) j -> p t j", p=P)
+
+        def load_base(h, tag):
+            base_sb[h] = kept([P, ROWT, HALF], F32, "base%d" % h, tag=tag)
+            nc.sync.dma_start(base_sb[h][:], base_rows[:, :, h * HALF : (h + 1) * HALF])
+
+        load_page(0, "page0")
+        wgs_sb = kept([P, S], F32, "wgs_sb", tag="wgs_x1")
+        nc.sync.dma_start(wgs_sb[:, 0:HALF], wgs[:, 0:HALF])
+        load_wd_early(1)
+        nc.sync.dma_start(wgs_sb[:, HALF:S], wgs[:, HALF:S])
 
         ident_bf = kept([P, P], BF16, "ident_bf")
         make_identity(nc, ident_bf[:])
         ident_f = kept([P, P], F32, "ident_f")
         make_identity(nc, ident_f[:])
 
+        v_w = [[None, None], [None, None]]
+
+        def picked(a, c0, c1):
+            h = c0 // HALF
+            return v_w[a][h][:, c0 - h * HALF : c1 - h * HALF]
+
+        def pick_words(a, c0, c1, tag=""):
+            if c0 % HALF == 0:
+                v_w[a][c0 // HALF] = kept([P, HALF], U32, "v_w%d_%d" % (a, c0 // HALF), tag=tag)
+            nc.vector.tensor_copy(picked(a, c0, c1), tab_w[a][:].bitcast(U32).indirect(entries(idx, c0, c1)))
+
+        pick_words(0, 0, HALF)
         v_sc = kept([P, S], U8, "v_sc")
         nc.vector.tensor_copy(v_sc[:], tab_sc[:].indirect(idx[:]))
         nc.scalar.dma_start(v_sc1[0:112, :].bitcast(I32), v_sc[4:116, :].bitcast(I32))
-        v_w = [[kept([P, HALF], U32, "v_w%d_%d" % (a, h)) for h in range(2)] for a in range(PASSES)]
-        for a in range(PASSES):
-            for h in range(2):
-                nc.vector.tensor_copy(v_w[a][h][:], tab_w[a][:].bitcast(U32).indirect(half_of(idx, h)))
+        pick_words(1, 0, QUARTER)
+        pick_words(1, QUARTER, HALF)
+        pick_words(0, HALF, S, tag="tab_sc")
+        pick_words(1, HALF, S)
 
         def interleave(dst, src):
             nc.scalar.copy(
@@ -119,31 +145,34 @@ def tile_list_surge_margin_page_kernel(
             nc.vector.quantize_mx(out=codes[:].bitcast(FP8X4), scales=scales[:], in_=src)
             return codes, scales
 
-        def sums(t, h, wd_c, wd_s):
-            cols = slice(h * HALF, (h + 1) * HALF)
-            den = psum.tile([P, HALF], F32, name="den", tag="acc_a")
+        def den_sum(t, c0, c1):
+            wd_c, wd_s = wd_q[t]
+            den = psum.tile([P, c1 - c0], F32, name="den", tag="acc_a")
             for a in range(PASSES):
                 nc.tensor.matmul_mx(
                     out=den[:],
                     lhsT=wd_c[:, a * P : (a + 1) * P].bitcast(FP8X4),
                     lhsT_scale=wd_s[:, a * P : (a + 1) * P],
-                    rhs=v_w[a][h][:].bitcast(FP8X4),
-                    rhs_scale=v_sc[4 * a : P, cols],
+                    rhs=picked(a, c0, c1).bitcast(FP8X4),
+                    rhs_scale=v_sc[4 * a : P, c0:c1],
                     start=(a == 0),
                     stop=(a == PASSES - 1),
                 )
-            num = psum.tile([P, HALF], F32, name="num", tag="acc_b")
+            return den
+
+        def num_sum(t, c0, c1):
+            num = psum.tile([P, c1 - c0], F32, name="num", tag="acc_b")
             for a in range(PASSES):
                 nc.tensor.matmul_mx(
                     out=num[:],
                     lhsT=wn_w[:, a, 2 * t * P : 2 * (t + 1) * P].bitcast(FP4X4),
                     lhsT_scale=wn_sc[:, a, t * P : (t + 1) * P],
-                    rhs=v_w[a][h][:].bitcast(FP8X4),
-                    rhs_scale=(v_sc, v_sc1)[a][:, cols],
+                    rhs=picked(a, c0, c1).bitcast(FP8X4),
+                    rhs_scale=(v_sc, v_sc1)[a][:, c0:c1],
                     start=(a == 0),
                     stop=(a == PASSES - 1),
                 )
-            return num, den
+            return num
 
         def halves(tile):
             return [tile[:, h * HALF : (h + 1) * HALF] for h in range(2)]
@@ -151,6 +180,7 @@ def tile_list_surge_margin_page_kernel(
         x = [[None] * ROWT, [None] * ROWT]
         z = [kept([P, ROWT, HALF], BF16, "z0"), None]
         turned = [None, None]
+        z_t = [None, None]
 
         def fetch(t, h, dst):
             x[h][t] = dst
@@ -164,15 +194,17 @@ def tile_list_surge_margin_page_kernel(
                 for b in range(2):
                     j0 = (2 * g + b) * P
                     nc.tensor.transpose(turned[g][:, b, t * P : (t + 1) * P], z[h][:, t, j0 : j0 + P], ident_bf[:])
+                if t == ROWT - 2:
+                    z_t[g] = ring.tile([P, 2, H], BF16, name="z_t", align_bytes=64)
+                    nc.scalar.copy(z_t[g][:, :, 0 : H - P], turned[g][:, :, 0 : H - P])
 
         def regroup(h):
             z_il = kept([P, HALF * PACK], BF16, "z_il%d" % h)
             for g in range(2):
-                z_t = ring.tile([P, 2, H], BF16, name="z_t", align_bytes=64)
-                nc.scalar.copy(z_t[:], turned[g][:])
+                nc.scalar.copy(z_t[g][:, :, H - P : H], turned[g][:, :, H - P : H])
                 back = psum.tile([P, 2, 2, P], F32, name="back", tag="back")
                 for b in range(2):
-                    words = z_t[:, b, :].bitcast(F32)
+                    words = z_t[g][:, b, :].bitcast(F32)
                     for u in range(2):
                         nc.tensor.transpose(back[:, b, u, :], words[:, u : H // 2 : 2], ident_f[:])
                 nc.scalar.copy(
@@ -181,39 +213,75 @@ def tile_list_surge_margin_page_kernel(
                 )
             return quantise(z_il[:], HALF, "z%d" % h)
 
+        def quantise_wd(t, flat):
+            nc.scalar.copy(
+                flat.rearrange("p (a c i j) -> p a c j i", a=PASSES, i=4, j=PACK),
+                wd_raw[t].rearrange("p a j (c i) -> p a c j i", i=4),
+            )
+            return quantise(flat, PASSES * P, "wd%d" % t)
+
+        wd_q = [quantise_wd(0, kept([P, PASSES * P * PACK], BF16, "wd_bf0")[:])]
+        wd_late = kept([P, PASSES, PACK, 2 * P], F32, "wd_late", tag="tab1")
+        for a in range(PASSES):
+            nc.sync.dma_start(wd_late[:, a, :, :], wd_rows[a, :, :, 2 * P : H])
+        for t in range(2):
+            wd_raw.append(wd_late[:, :, :, t * P : (t + 1) * P])
+
         for t in range(ROWT):
-            wd_bf = ring.tile([P, PASSES, P, PACK], BF16, name="wd_bf", align_bytes=64)
-            for a in range(PASSES):
-                interleave(wd_bf[:, a, :, :], wd_raw[t // 2][a][:, :, (t % 2) * P : (t % 2 + 1) * P])
-            wd_c, wd_s = quantise(wd_bf[:].rearrange("p a c j -> p (a c j)"), PASSES * P, "wd%d" % t)
-            hh = ring.tile([P, S], F32, name="hh")
-            mag = ring.tile([P, S], F32, name="mag")
-            root = ring.tile([P, S], F32, name="root")
+            root = kept([P, S], F32, "root%d" % t, tag="work%d" % (t + 2))
             recip = kept([P, S], F32, "recip%d" % t)
             if t == 0:
-                for h in range(2):
-                    num, den = sums(t, h, wd_c, wd_s)
-                    nc.scalar.activation(halves(mag)[h], den[:], ACT.Abs)
-                    nc.scalar.activation(halves(root)[h], halves(mag)[h], ACT.Abs_reciprocal_sqrt, bias=1.0)
-                    nc.scalar.activation(halves(recip)[h], halves(root)[h], ACT.Square)
-                    nc.vector.tensor_tensor(halves(hh)[h], num[:], halves(recip)[h], ALU.mult)
+                hh = ring.tile([P, S], F32, name="hh", align_bytes=64)
+                between = (
+                    (root[:, 0:QUARTER], root[:, QUARTER:HALF]),
+                    (root[:, QUARTER:HALF], hh[:, HALF : HALF + QUARTER]),
+                    (root[:, 0:HALF], root[:, HALF:S]),
+                )
+                dens = [den_sum(t, c0, c1) for c0, c1 in FIRST_CUTS[:2]]
+                for n, (c0, c1) in enumerate(FIRST_CUTS):
+                    if n == 1:
+                        dens.append(den_sum(t, HALF, S))
+                    num = num_sum(t, c0, c1)
+                    first, second = between[n]
+                    nc.scalar.activation(first, dens[n][:], ACT.Abs)
+                    nc.scalar.activation(second, first, ACT.Abs_reciprocal_sqrt, bias=1.0)
+                    nc.scalar.activation(recip[:, c0:c1], second, ACT.Square)
+                    if n == 2:
+                        wd_q.append(quantise_wd(1, hh[:, HALF:S].bitcast(BF16)))
+                    nc.vector.tensor_tensor(hh[:, c0:c1], num[:], recip[:, c0:c1], ALU.mult)
                     nc.vector.tensor_tensor(
-                        pages[t][:].indirect(half_of(idx2, h)), halves(hh)[h], halves(wgs_sb)[h], ALU.mult
+                        pages[t][:].indirect(entries(idx2, c0, c1)), hh[:, c0:c1], wgs_sb[:, c0:c1], ALU.mult
                     )
+                load_page(1, "wd0_codes")
+                load_page(2, "recip0")
+                first_root = root
             else:
-                nums = []
+                dens = [den_sum(t, c0, c1) for c0, c1 in HALVES]
+                nums = [num_sum(t, c0, c1) for c0, c1 in HALVES]
+                mag = first_root if t == 1 else kept([P, S], F32, "mag%d" % t, tag="mag%d" % t)
                 for h in range(2):
-                    num, den = sums(t, h, wd_c, wd_s)
-                    nums.append(num)
-                    nc.scalar.activation(halves(mag)[h], den[:], ACT.Abs)
+                    nc.scalar.activation(halves(mag)[h], dens[h][:], ACT.Abs)
                 nc.scalar.activation(root[:], mag[:], ACT.Abs_reciprocal_sqrt, bias=1.0)
                 nc.scalar.activation(recip[:], root[:], ACT.Square)
+                hh = ring.tile([P, S], F32, name="hh", align_bytes=64)
+                if t + 1 < ROWT:
+                    staged = kept([P, PASSES * P * PACK], BF16, "wd_bf%d" % (t + 1), tag=("work2", "mag2")[t - 1])
+                    wd_q.append(quantise_wd(t + 1, staged[:]))
+                if t == 1:
+                    load_base(0, "wd1_codes")
+                if t == 2:
+                    load_page(3, "tab1")
                 for h in range(2):
                     nc.vector.tensor_tensor(halves(hh)[h], nums[h][:], halves(recip)[h], ALU.mult)
                 fetch(t - 1, 0, halves(recip)[0])
                 nc.vector.tensor_tensor(pages[t][:].indirect(idx2[:]), hh[:], wgs_sb[:], ALU.mult)
                 hold_up(t - 1, 0)
 
+        wr_raw = kept([P, PACK, H], F32, "wr_raw", tag="wn_wr")
+        nc.sync.dma_start(wr_raw[:], wr.rearrange("(p j) c -> p j c", j=PACK))
+        load_base(1, "v_w1_1")
+        wgo_sb = kept([P, NP], F32, "wgo_sb", tag="tab_sc")
+        nc.sync.dma_start(wgo_sb[:], wgo)
         wr_bf = kept([P, H, PACK], BF16, "wr_bf")
         interleave(wr_bf[:], wr_raw[:])
         wr_c, wr_s = quantise(wr_bf[:].rearrange("p c j -> p (c j)"), H, "wr")

@@ -58,6 +58,10 @@ def tile_list_surge_margin_page_kernel(
         v_sc1 = kept([P, S], U8, "v_sc1")
         nc.vector.memset(v_sc1[:].bitcast(I32), 0)
 
+        warm = kept([P, 2], F32, "warm")
+        nc.gpsimd.memset(warm[:, 0:1], 1.0)
+        nc.scalar.activation(warm[:, 1:2], warm[:, 0:1], ACT.Abs_reciprocal_sqrt, bias=1.0)
+
         idx = load_list(offs, "idx")
         for q in range(4):
             nc.sync.dma_start(

from contextlib import ExitStack

import concourse.mybir as mybir
from concourse.masks import make_identity

K, H, T, S, T2, NP = 1024, 512, 2048, 1024, 2048, 1024
FLOPS = 2 * (2 * K * H * S) + 2 * H * H * NP

F32 = mybir.dt.float32
BF16 = mybir.dt.bfloat16
I32 = mybir.dt.int32
U32 = mybir.dt.uint32
U16 = mybir.dt.uint16
U8 = mybir.dt.uint8
FP8X4 = mybir.dt.float8_e4m3fn_x4
FP4X4 = mybir.dt.float4_e2m1fn_x4
ACT = mybir.ActivationFunctionType
ALU = mybir.AluOpType

P = 128
PACK = 4
PASSES = K // (P * PACK)
ROWT = H // P
HALF = 512
QUARTER = HALF // 2
HALVES = ((0, HALF), (HALF, S))
FIRST_CUTS = ((0, QUARTER), (QUARTER, HALF), (HALF, S))


def tile_list_surge_margin_page_kernel(
    tc, tab_words, tab_scales, offs, wn_words, wn_scales, wd, page0, wgs, offs2, offs3, base, wr, wgo, offs4, out
):
    nc = tc.nc
    with ExitStack() as ctx:
        lists = ctx.enter_context(tc.tile_pool(name="lists", bufs=1))
        keep = ctx.enter_context(tc.tile_pool(name="keep", bufs=1))
        ring = ctx.enter_context(tc.tile_pool(name="ring", bufs=2))
        psum = ctx.enter_context(tc.psum_pool(name="psum", bufs=2))

        def kept(shape, dtype, name, tag=""):
            return keep.tile(shape, dtype, name=name, tag=tag or name, align_bytes=64)

        def load_list(src, name):
            tile = lists.tile([P, S // 16], U16, name=name)
            nc.sync.dma_start(tile[:], src)
            return tile

        def entries(lst, c0, c1):
            return lst[:, c0 // 16 : c1 // 16]

        def half_of(lst, h):
            return entries(lst, h * HALF, (h + 1) * HALF)

        tab_sc = kept([P, T], U8, "tab_sc")
        nc.vector.memset(tab_sc[:].bitcast(I32), 0)
        wn_sc = kept([P, PASSES, H], U8, "wn_sc")
        nc.vector.memset(wn_sc[:].rearrange("p a c -> p (a c)").bitcast(I32), 0)
        v_sc1 = kept([P, S], U8, "v_sc1")
        nc.vector.memset(v_sc1[:].bitcast(I32), 0)

        warm = kept([P, 2], F32, "warm")
        nc.gpsimd.memset(warm[:, 0:1], 1.0)
        nc.scalar.activation(warm[:, 1:2], warm[:, 0:1], ACT.Abs_reciprocal_sqrt, bias=1.0)

        idx = load_list(offs, "idx")
        for q in range(4):
            nc.sync.dma_start(
                tab_sc[32 * q : 32 * q + 8, :].bitcast(I32), tab_scales[:, 4 * q : 4 * q + 4, :].bitcast(I32)
            )
        idx2 = load_list(offs2, "idx2")
        idx3 = load_list(offs3, "idx3")
        idx4 = load_list(offs4, "idx4")
        wn_w = kept([P, PASSES, 2 * H], U8, "wn_w", tag="wn_wr")
        tab_w = [kept([P, T], I32, "tab_w%d" % a, tag="tab%d" % a) for a in range(PASSES)]
        wd_rows = wd.rearrange("(a p j) c -> a p j c", a=PASSES, j=PACK)
        wd_raw = [kept([P, PASSES, PACK, P], F32, "wd_raw%d" % t)[:] for t in range(2)]

        def load_wd_early(t):
            for a in range(PASSES):
                nc.sync.dma_start(wd_raw[t][:, a, :, :], wd_rows[a, :, :, t * P : (t + 1) * P])

        def load_wn(a):
            nc.sync.dma_start(wn_w[:, a, :].bitcast(I32), wn_words[a].bitcast(I32))

        nc.sync.dma_start(tab_w[0][:], tab_words[0].rearrange("p t i -> p (t i)").bitcast(I32))
        load_wd_early(0)
        load_wn(0)
        nc.sync.dma_start(tab_w[1][:], tab_words[1].rearrange("p t i -> p (t i)").bitcast(I32))
        for q in range(4):
            nc.sync.dma_start(
                wn_sc[32 * q : 32 * q + 4, :, :].bitcast(I32),
                wn_scales[:, 4 * q : 4 * q + 4, :].rearrange("a r c -> r a c").bitcast(I32),
            )

        load_wn(1)
        pages = [None] * ROWT

        def load_page(t, tag):
            pages[t] = kept([P, T2], F32, "page%d" % t, tag=tag)
            nc.sync.dma_start(pages[t][:], page0[t * P : (t + 1) * P, :])

        base_sb = [None, None]
        base_rows = base.rearrange("(t p) j -> p t j", p=P)

        def load_base(h, tag):
            base_sb[h] = kept([P, ROWT, HALF], F32, "base%d" % h, tag=tag)
            nc.sync.dma_start(base_sb[h][:], base_rows[:, :, h * HALF : (h + 1) * HALF])

        load_page(0, "page0")
        wgs_sb = kept([P, S], F32, "wgs_sb", tag="wgs_x1")
        nc.sync.dma_start(wgs_sb[:, 0:HALF], wgs[:, 0:HALF])
        load_wd_early(1)
        nc.sync.dma_start(wgs_sb[:, HALF:S], wgs[:, HALF:S])

        ident_bf = kept([P, P], BF16, "ident_bf")
        make_identity(nc, ident_bf[:])
        ident_f = kept([P, P], F32, "ident_f")
        make_identity(nc, ident_f[:])

        v_w = [[None, None], [None, None]]

        def picked(a, c0, c1):
            h = c0 // HALF
            return v_w[a][h][:, c0 - h * HALF : c1 - h * HALF]

        def pick_words(a, c0, c1, tag=""):
            if c0 % HALF == 0:
                v_w[a][c0 // HALF] = kept([P, HALF], U32, "v_w%d_%d" % (a, c0 // HALF), tag=tag)
            nc.vector.tensor_copy(picked(a, c0, c1), tab_w[a][:].bitcast(U32).indirect(entries(idx, c0, c1)))

        pick_words(0, 0, HALF)
        v_sc = kept([P, S], U8, "v_sc")
        nc.vector.tensor_copy(v_sc[:], tab_sc[:].indirect(idx[:]))
        nc.scalar.dma_start(v_sc1[0:112, :].bitcast(I32), v_sc[4:116, :].bitcast(I32))
        pick_words(1, 0, QUARTER)
        pick_words(1, QUARTER, HALF)
        pick_words(0, HALF, S, tag="tab_sc")
        pick_words(1, HALF, S)

        def interleave(dst, src):
            nc.scalar.copy(
                dst.rearrange("p (c i) j -> p c j i", i=4),
                src.rearrange("p j (c i) -> p c j i", i=4),
            )

        def quantise(src, width, name):
            codes = kept([P, width], U32, name + "_codes")
            scales = kept([P, width], U8, name + "_scales")
            nc.vector.quantize_mx(out=codes[:].bitcast(FP8X4), scales=scales[:], in_=src)
            return codes, scales

        def den_sum(t, c0, c1):
            wd_c, wd_s = wd_q[t]
            den = psum.tile([P, c1 - c0], F32, name="den", tag="acc_a")
            for a in range(PASSES):
                nc.tensor.matmul_mx(
                    out=den[:],
                    lhsT=wd_c[:, a * P : (a + 1) * P].bitcast(FP8X4),
                    lhsT_scale=wd_s[:, a * P : (a + 1) * P],
                    rhs=picked(a, c0, c1).bitcast(FP8X4),
                    rhs_scale=v_sc[4 * a : P, c0:c1],
                    start=(a == 0),
                    stop=(a == PASSES - 1),
                )
            return den

        def num_sum(t, c0, c1):
            num = psum.tile([P, c1 - c0], F32, name="num", tag="acc_b")
            for a in range(PASSES):
                nc.tensor.matmul_mx(
                    out=num[:],
                    lhsT=wn_w[:, a, 2 * t * P : 2 * (t + 1) * P].bitcast(FP4X4),
                    lhsT_scale=wn_sc[:, a, t * P : (t + 1) * P],
                    rhs=picked(a, c0, c1).bitcast(FP8X4),
                    rhs_scale=(v_sc, v_sc1)[a][:, c0:c1],
                    start=(a == 0),
                    stop=(a == PASSES - 1),
                )
            return num

        def halves(tile):
            return [tile[:, h * HALF : (h + 1) * HALF] for h in range(2)]

        x = [[None] * ROWT, [None] * ROWT]
        z = [kept([P, ROWT, HALF], BF16, "z0"), None]
        turned = [None, None]
        z_t = [None, None]

        def fetch(t, h, dst):
            x[h][t] = dst
            nc.vector.tensor_copy(dst, pages[t][:].indirect(half_of(idx3, h)))

        def hold_up(t, h):
            nc.vector.tensor_tensor(z[h][:, t, :], x[h][t], base_sb[h][:, t, :], ALU.max)
            for g in range(2):
                if t == 0:
                    turned[g] = psum.tile([P, 2, H], BF16, name="turned", tag="turned")
                for b in range(2):
                    j0 = (2 * g + b) * P
                    nc.tensor.transpose(turned[g][:, b, t * P : (t + 1) * P], z[h][:, t, j0 : j0 + P], ident_bf[:])
                if t == ROWT - 2:
                    z_t[g] = ring.tile([P, 2, H], BF16, name="z_t", align_bytes=64)
                    nc.scalar.copy(z_t[g][:, :, 0 : H - P], turned[g][:, :, 0 : H - P])

        def regroup(h):
            z_il = kept([P, HALF * PACK], BF16, "z_il%d" % h)
            for g in range(2):
                nc.scalar.copy(z_t[g][:, :, H - P : H], turned[g][:, :, H - P : H])
                back = psum.tile([P, 2, 2, P], F32, name="back", tag="back")
                for b in range(2):
                    words = z_t[g][:, b, :].bitcast(F32)
                    for u in range(2):
                        nc.tensor.transpose(back[:, b, u, :], words[:, u : H // 2 : 2], ident_f[:])
                nc.scalar.copy(
                    z_il[:, g * 1024 : (g + 1) * 1024].bitcast(F32).rearrange("p (b j u) -> p b j u", b=2, u=2),
                    back[:].rearrange("p b u j -> p b j u"),
                )
            return quantise(z_il[:], HALF, "z%d" % h)

        def quantise_wd(t, flat):
            nc.scalar.copy(
                flat.rearrange("p (a c i j) -> p a c j i", a=PASSES, i=4, j=PACK),
                wd_raw[t].rearrange("p a j (c i) -> p a c j i", i=4),
            )
            return quantise(flat, PASSES * P, "wd%d" % t)

        wd_q = [quantise_wd(0, kept([P, PASSES * P * PACK], BF16, "wd_bf0")[:])]
        wd_late = kept([P, PASSES, PACK, 2 * P], F32, "wd_late", tag="tab1")
        for a in range(PASSES):
            nc.sync.dma_start(wd_late[:, a, :, :], wd_rows[a, :, :, 2 * P : H])
        for t in range(2):
            wd_raw.append(wd_late[:, :, :, t * P : (t + 1) * P])

        for t in range(ROWT):
            root = kept([P, S], F32, "root%d" % t, tag="work%d" % (t + 2))
            recip = kept([P, S], F32, "recip%d" % t)
            if t == 0:
                hh = ring.tile([P, S], F32, name="hh", align_bytes=64)
                between = (
                    (root[:, 0:QUARTER], root[:, QUARTER:HALF]),
                    (root[:, QUARTER:HALF], hh[:, HALF : HALF + QUARTER]),
                    (root[:, 0:HALF], root[:, HALF:S]),
                )
                dens = [den_sum(t, c0, c1) for c0, c1 in FIRST_CUTS[:2]]
                for n, (c0, c1) in enumerate(FIRST_CUTS):
                    if n == 1:
                        dens.append(den_sum(t, HALF, S))
                    num = num_sum(t, c0, c1)
                    first, second = between[n]
                    nc.scalar.activation(first, dens[n][:], ACT.Abs)
                    nc.scalar.activation(second, first, ACT.Abs_reciprocal_sqrt, bias=1.0)
                    nc.scalar.activation(recip[:, c0:c1], second, ACT.Square)
                    if n == 2:
                        wd_q.append(quantise_wd(1, hh[:, HALF:S].bitcast(BF16)))
                    nc.vector.tensor_tensor(hh[:, c0:c1], num[:], recip[:, c0:c1], ALU.mult)
                    nc.vector.tensor_tensor(
                        pages[t][:].indirect(entries(idx2, c0, c1)), hh[:, c0:c1], wgs_sb[:, c0:c1], ALU.mult
                    )
                load_page(1, "wd0_codes")
                load_page(2, "recip0")
                first_root = root
            else:
                dens = [den_sum(t, c0, c1) for c0, c1 in HALVES]
                nums = [num_sum(t, c0, c1) for c0, c1 in HALVES]
                mag = first_root if t == 1 else kept([P, S], F32, "mag%d" % t, tag="mag%d" % t)
                for h in range(2):
                    nc.scalar.activation(halves(mag)[h], dens[h][:], ACT.Abs)
                nc.scalar.activation(root[:], mag[:], ACT.Abs_reciprocal_sqrt, bias=1.0)
                nc.scalar.activation(recip[:], root[:], ACT.Square)
                hh = ring.tile([P, S], F32, name="hh", align_bytes=64)
                if t + 1 < ROWT:
                    staged = kept([P, PASSES * P * PACK], BF16, "wd_bf%d" % (t + 1), tag=("work2", "mag2")[t - 1])
                    wd_q.append(quantise_wd(t + 1, staged[:]))
                if t == 1:
                    load_base(0, "wd1_codes")
                if t == 2:
                    load_page(3, "tab1")
                for h in range(2):
                    nc.vector.tensor_tensor(halves(hh)[h], nums[h][:], halves(recip)[h], ALU.mult)
                fetch(t - 1, 0, halves(recip)[0])
                nc.vector.tensor_tensor(pages[t][:].indirect(idx2[:]), hh[:], wgs_sb[:], ALU.mult)
                hold_up(t - 1, 0)

        wr_raw = kept([P, PACK, H], F32, "wr_raw", tag="wn_wr")
        nc.sync.dma_start(wr_raw[:], wr.rearrange("(p j) c -> p j c", j=PACK))
        load_base(1, "v_w1_1")
        wgo_sb = kept([P, NP], F32, "wgo_sb", tag="tab_sc")
        nc.sync.dma_start(wgo_sb[:], wgo)
        wr_bf = kept([P, H, PACK], BF16, "wr_bf")
        interleave(wr_bf[:], wr_raw[:])
        wr_c, wr_s = quantise(wr_bf[:].rearrange("p c j -> p (c j)"), H, "wr")

        x_last = kept([P, HALF], F32, "x_last")
        x_late = kept([P, ROWT, HALF], F32, "x_late", tag="wgs_x1")
        fetch(ROWT - 1, 0, x_last[:])
        fetch(0, 1, x_late[:, 0, :])
        hold_up(ROWT - 1, 0)
        for t in range(1, ROWT):
            fetch(t, 1, x_late[:, t, :])
        zq = [regroup(0), None]
        z[1] = kept([P, ROWT, HALF], BF16, "z1", tag="z_il0")
        for t in range(ROWT):
            hold_up(t, 1)

        lows = [kept([P, NP], F32, "low%d" % t) for t in range(ROWT)]

        def rescore(t, h):
            z_c, z_s = zq[h]
            y = psum.tile([P, HALF], F32, name="y", tag=("acc_a", "acc_b")[t % 2])
            nc.tensor.matmul_mx(
                out=y[:],
                lhsT=wr_c[:, t * P : (t + 1) * P].bitcast(FP8X4),
                lhsT_scale=wr_s[:, t * P : (t + 1) * P],
                rhs=z_c[:].bitcast(FP8X4),
                rhs_scale=z_s[:],
                start=True,
                stop=True,
            )
            nc.vector.tensor_tensor(halves(lows[t])[h], y[:], x[h][t], ALU.min)

        def put_first_tile(h):
            nc.vector.tensor_tensor(
                pages[0][:].indirect(half_of(idx4, h)), halves(lows[0])[h], halves(wgo_sb)[h], ALU.mult
            )

        def store(t):
            nc.sync.dma_start(out[t * P : (t + 1) * P, :], pages[t][:])

        rescore(0, 0)
        rescore(1, 0)
        put_first_tile(0)
        zq[1] = regroup(1)
        rescore(2, 0)
        rescore(3, 0)
        rescore(0, 1)
        rescore(1, 1)
        put_first_tile(1)
        store(0)
        for t in range(1, ROWT):
            if t + 1 < ROWT:
                rescore(t + 1, 1)
            nc.vector.tensor_tensor(pages[t][:].indirect(idx4[:]), lows[t][:], wgo_sb[:], ALU.mult)
            store(t)
